import numpy as np, ml_dtypes
CORES = [29,45,93,109,157,173,221,237,285,301,349,365,413,429,477,493]
N = 16
import mx_ref
NC, G = 256, 2
C, C2 = np.float32(0.043), np.float32(0.041)
CNT = [[16,16,16,16,16,16,16,16,16,16,16,16,16,16,16,16],[16,16,16,16,16,16,16,16,16,16,16,16,16,16,16,16],[16,16,16,16,16,16,16,16,16,16,16,16,16,16,16,16],[16,16,16,16,16,16,16,16,16,16,16,16,16,16,16,16],[16,16,16,16,16,16,16,16,16,16,16,16,16,16,16,16],[16,16,16,16,16,16,16,16,16,16,16,16,16,16,16,16],[16,16,16,16,16,16,16,16,16,16,16,16,16,16,16,16],[16,16,16,16,16,16,16,16,16,16,16,16,16,16,16,16],[16,16,16,16,16,16,16,16,16,16,16,16,16,16,16,16],[16,16,16,16,16,16,16,16,16,16,16,16,16,16,16,16],[16,16,16,16,16,16,16,16,16,16,16,16,16,16,16,16],[16,16,16,16,16,16,16,16,16,16,16,16,16,16,16,16],[16,16,16,16,16,16,16,16,16,16,16,16,16,16,16,16],[16,16,16,16,16,16,16,16,16,16,16,16,16,16,16,16],[16,16,16,16,16,16,16,16,16,16,16,16,16,16,16,16],[16,16,16,16,16,16,16,16,16,16,16,16,16,16,16,16]]
OFF = [[sum(c[:e]) for e in range(N + 1)] for c in CNT]
BF = ml_dtypes.bfloat16
def cut(t, i, w=512):
    return t[:, w * i:w * i + w]
def tile(rs):
    return np.stack(rs, axis=2).reshape(128, -1).astype(BF)
def layer(w, X):
    out = []
    for i in range(G):
        for t in range(len(X)):
            p = mx_ref.matmul(mx_ref.quantize(cut(w, len(X) * i + t)), X[t])
            z = p if t == 0 else z + p
        out.append(z)
    return out
def act(Z):
    return [np.maximum(s * z, 0) * C for z in Z for s in (1, -1)]
def setup_inputs(rng):
    def f(*shape):
        return mx_ref.flush((rng.standard_normal(shape, dtype=np.float32) * np.exp2(rng.integers(-2, 3, shape[:-1] + (1,)))).astype(BF))
    return {"x": f(N, 128, 4 * NC), "w1": f(N, 128, G * 512), "w2": f(N, 128, G * 512), "w3": f(N, 128, 512)}
def setup_inputs_blocks(rng):
    d = setup_inputs(rng)
    for k in ("x", "w3"): d[k] = mx_ref.spread(d[k], rng, 4)
    for k in ("w1", "w2"): d[k] = mx_ref.spread(d[k], rng, 2)
    return d
def setup_inputs_wide(rng):
    d = setup_inputs(rng)
    for k in ("x", "w1", "w2", "w3"): d[k] = mx_ref.flush((d[k].astype(np.float32) * np.exp2(rng.integers(-4, 5, (N, 1, 1))).astype(np.float32)).astype(BF))
    return d
def setup_inputs_zeros(rng):
    d = setup_inputs(rng); v = d["x"].reshape(N, 128, -1, 4).copy()
    v[np.broadcast_to((rng.random((N, 1, v.shape[2], 1)) < 0.33), v.shape)] = 0
    d["x"] = v.reshape(d["x"].shape)
    return d
def act2(Z):
    return [np.maximum(s * z, 0) * C2 for z in Z for s in (1, -1)]
def reference(x, w1, w2, w3):
    h = [tile(act(layer(w1[j], [mx_ref.quantize(x[j])]))) for j in range(N)]
    g = []
    for e in range(N):
        t = np.concatenate([h[j][:, 4 * OFF[j][e]:4 * OFF[j][e + 1]] for j in range(N)], axis=1)
        g.append(tile(act2(layer(w2[e], [mx_ref.quantize(t)]))))
    y = np.zeros((N, 128, NC), np.float32)
    for j in range(N):
        back = []
        for e in range(N):
            a = sum(CNT[i][e] for i in range(j))
            back.append(g[e][:, 4 * a:4 * a + 4 * CNT[j][e]])
        y[j] = mx_ref.matmul(mx_ref.quantize(w3[j]), mx_ref.quantize(np.concatenate(back, axis=1)))
    return {"y": y}

@@ -1,0 +1,226 @@
+from concourse.bass import DstId, RemoteDMATransfer
+from concourse.mybir import dt, AluOpType, ActivationFunctionType
+
+SIM = 512
+W = 16
+H = 128
+OWN1 = H - W
+IN1 = H
+CR1 = IN1 + H - W
+PK2 = H - W
+C1, C2 = 0.043, 0.041
+
+X4 = "float8_e4m3fn_x4"
+SCRATCH = {
+    "xa": ("sbuf", [128, 4 * H], "bfloat16"), "xb": ("sbuf", [128, 4 * H], "bfloat16"),
+    "t10": ("sbuf", [128, 512], "bfloat16"), "t11": ("sbuf", [128, 512], "bfloat16"),
+    "t2": ("sbuf", [128, 1024], "bfloat16"), "t3": ("sbuf", [128, 512], "bfloat16"),
+    "ha": ("sbuf", [128, 4 * H], "bfloat16"), "hb": ("sbuf", [128, 4 * H], "bfloat16"),
+    "ge": ("sbuf", [128, 4 * H], "bfloat16"), "gx": ("sbuf", [128, 4 * H], "bfloat16"),
+    "yt": ("sbuf", [128, 256], "float32"),
+    "ps": ("psum", [128, 512 * 8], "float32"),
+}
+for _n, _w in (("xa", H), ("xb", H), ("w1", 256), ("w2", 256), ("w3", 128), ("ha", H), ("b", CR1 + H), ("c", PK2 + H),
+               ("gx", H), ("e", H), ("r1", 64), ("r2", 64)):
+    SCRATCH["k_" + _n] = ("sbuf", [128, _w], X4)
+    SCRATCH["s_" + _n] = ("sbuf", [128, _w], "uint8")
+
+SEMAPHORES = ["lxa", "lxb", "lw10", "lw11", "lw2", "lw3", "qw10", "qw11", "qxa", "qxb", "qw2", "qw3",
+              "za0", "za1", "zb0", "zb1", "ze0", "ze1", "zc0", "zc1", "ta", "tb", "te", "tc", "qha", "qhb", "qge", "qgx",
+              "in1", "cr1", "in2", "cr2", "fe", "fc", "ye", "yc", "out", "sent", "hop1", "hop2"]
+
+PLAN = {}
+
+
+def plan(T, topo):
+    if PLAN:
+        return PLAN
+    cores = [int(c) for c in T.cores]
+    ranks = range(len(cores))
+    rk = [topo.rack(topo.host(c)) for c in cores]
+    mine = [[r for r in ranks if rk[r] == rk[j]] for j in ranks]
+    far = [[r for r in ranks if rk[r] != rk[j]] for j in ranks]
+    ring, blocks, relay = [], [], {}
+    for j in ranks:
+        i = mine[j].index(j)
+        ring.append(mine[j][i + 1:] + mine[j][:i])
+        near = [r for r in far[j] if topo.may_write(cores[j], cores[r])]
+        diag = [r for r in far[j] if r not in near]
+        peer = [cores[r] for r in near if topo.chip(cores[r]) == topo.chip(cores[j])][0]
+        help_ = [c for c in range(SIM) if topo.host(c) == topo.host(peer) and topo.chip(c) == topo.chip(peer)
+                 and topo.die(c) != topo.die(peer) and T.rank_of(c) is None]
+        bl = []
+        for n, dests in enumerate((diag, near)):
+            kc, sc = help_[2 * n], help_[2 * n + 1]
+            relay[kc] = (j, dests, True)
+            relay[sc] = (j, dests, False)
+            bl.append((far[j].index(dests[0]) * W, kc, sc))
+        blocks.append(bl)
+    PLAN.update(cores=cores, mine=mine, far=far, ring=ring, blocks=blocks, relay=relay)
+    return PLAN
+
+
+def view(T, codes, name, a, n):
+    if codes:
+        return T["k_" + name][:, a:a + n].bitcast(dt.uint8)
+    return T["s_" + name][:, a:a + n]
+
+
+def fused(g, core, T, topo, sem, moves):
+    m = 0xFFFF
+    for d, _, _ in moves:
+        m &= topo.mask(core, d)
+    eng = [i for i in range(16) if m >> i & 1]
+    per = 1
+    while 2 * per * len(moves) <= len(eng):
+        per *= 2
+    tr = []
+    for n, (d, src, dst) in enumerate(moves):
+        rid, pid = topo.addr(d, core)
+        tr.append(RemoteDMATransfer(dst_ids=[DstId(rid=rid, pnc=pid)],
+                                    dma_engine_mask=sum(1 << i for i in eng[n * per:n * per + per]),
+                                    remote_sem=sem, src=src, dst=dst))
+    g.remote_dma_fused(tr, local_sem=T.sem.sent)
+    return per * len(moves)
+
+
+def relay_program(g, core, T, topo, P):
+    j, dests, codes = P["relay"][core]
+    at = W * P["mine"][j].index(j)
+    sent = 0
+    for hop, land, buf, base, sem in ((T.sem.hop1, "r1", "b", CR1, T.sem.cr1), (T.sem.hop2, "r2", "e", 0, T.sem.cr2)):
+        g.wait_ge(hop, 4)
+        sent += fused(g, core, T, topo, sem, [(P["cores"][d], view(T, codes, land, W * n, W), view(T, codes, buf, base + at, W))
+                                              for n, d in enumerate(dests)])
+    g.wait_ge(T.sem.sent, sent)
+
+
+def rank_program(g, core, T, topo):
+    P = plan(T, topo)
+    rank = T.rank_of(core)
+    if rank is None:
+        if core in P["relay"]:
+            relay_program(g, core, T, topo, P)
+        return
+    S = T.sem
+    cores, ring = P["cores"], P["ring"][rank]
+    far0, mine0 = P["far"][rank][0], P["mine"][rank][0]
+    me = P["mine"][rank].index(rank)
+    tail = H - W * (me + 1)
+    V, TE, A, SY = g.vector, g.tensor, g.scalar, g.sync
+    mul, mx = AluOpType.mult, AluOpType.max
+    relu = ActivationFunctionType.Relu
+
+    A.dma_start(T.t10[:], T.w1[:, 0:512]).then_inc(S.lw10, 16)
+    SY.dma_start(T.xa[:], T.x[:, 4 * W * far0:4 * W * far0 + 4 * H]).then_inc(S.lxa, 16)
+    A.dma_start(T.t11[:], T.w1[:, 512:1024]).then_inc(S.lw11, 16)
+    x0 = 4 * W * mine0
+    nb = 16
+    if tail:
+        SY.dma_start(T.xb[:, 0:4 * tail], T.x[:, x0 + 4 * (H - tail):x0 + 4 * H]).then_inc(S.lxb, 16)
+        nb = 32
+    SY.dma_start(T.xb[:, 4 * tail:4 * H], T.x[:, x0:x0 + 4 * (H - tail)]).then_inc(S.lxb, 16)
+    SY.wait_ge(S.lw11, 16)
+    SY.wait_ge(S.lxb, nb)
+    SY.dma_start(T.t2[:], T.w2[:]).then_inc(S.lw2, 16)
+    SY.dma_start(T.t3[:], T.w3[:]).then_inc(S.lw3, 16)
+
+    def bank(b, n=H):
+        return T.ps[:, 512 * b:512 * b + n]
+
+    def quant(name, a, n, src, sem):
+        V.quantize_mx(T["k_" + name][:, a:a + n], T["s_" + name][:, a:a + n], src).then_inc(sem, 1)
+
+    def mm(b, w, wa, x, xa, sem):
+        TE.matmul_mx(bank(b), T["k_" + w][:, wa:wa + 128], T["s_" + w][:, wa:wa + 128],
+                     T["k_" + x][:, xa:xa + H], T["s_" + x][:, xa:xa + H], True, True).then_inc(sem, 1)
+
+    def acts(tile, b, z0, z1, c, done):
+        V.wait_ge(z0, 1)
+        V.tensor_scalar(tile[:, 0:4 * H:4], bank(b), c, 0.0, mul, mx).then_inc(done, 1)
+        V.tensor_scalar(tile[:, 1:4 * H:4], bank(b), -c, 0.0, mul, mx).then_inc(done, 1)
+        A.wait_ge(z1, 1)
+        A.activation(tile[:, 2:4 * H:4], bank(b + 1), relu, scale=c).then_inc(done, 1)
+        A.activation(tile[:, 3:4 * H:4], bank(b + 1), relu, scale=-c).then_inc(done, 1)
+        V.wait_ge(done, 4)
+
+    V.wait_ge(S.lw10, 16)
+    quant("w1", 0, 128, T.t10[:], S.qw10)
+    V.wait_ge(S.lxa, 16)
+    quant("xa", 0, H, T.xa[:], S.qxa)
+    V.wait_ge(S.lw11, 16)
+    quant("w1", 128, 128, T.t11[:], S.qw11)
+    TE.wait_ge(S.qw10, 1)
+    TE.wait_ge(S.qxa, 1)
+    mm(0, "w1", 0, "xa", 0, S.za0)
+    TE.wait_ge(S.qw11, 1)
+    mm(1, "w1", 128, "xa", 0, S.za1)
+    acts(T.ha, 0, S.za0, S.za1, C1, S.ta)
+    quant("ha", 0, H, T.ha[:], S.qha)
+    V.wait_ge(S.lxb, nb)
+    quant("xb", 0, H, T.xb[:], S.qxb)
+    TE.wait_ge(S.qxb, 1)
+    mm(2, "w1", 0, "xb", 0, S.zb0)
+    mm(3, "w1", 128, "xb", 0, S.zb1)
+    acts(T.hb, 2, S.zb0, S.zb1, C1, S.tb)
+    quant("b", 0, H, T.hb[:], S.qhb)
+    V.wait_ge(S.lw2, 16)
+    quant("w2", 0, 128, T.t2[:, 0:512], S.qw2)
+    quant("w2", 128, 128, T.t2[:, 512:1024], S.qw2)
+    V.wait_ge(S.lw3, 16)
+    quant("w3", 0, 128, T.t3[:], S.qw3)
+
+    TE.wait_ge(S.qw2, 2)
+    TE.wait_ge(S.qhb, 1)
+    TE.wait_ge(S.in1, 14)
+    mm(4, "w2", 0, "b", OWN1, S.ze0)
+    mm(5, "w2", 128, "b", OWN1, S.ze1)
+    acts(T.ge, 4, S.ze0, S.ze1, C2, S.te)
+    quant("c", PK2, H, T.ge[:], S.qge)
+    TE.wait_ge(S.cr1, 32)
+    mm(6, "w2", 0, "b", CR1, S.zc0)
+    mm(7, "w2", 128, "b", CR1, S.zc1)
+    acts(T.gx, 6, S.zc0, S.zc1, C2, S.tc)
+    quant("gx", 0, H, T.gx[:], S.qgx)
+
+    TE.wait_ge(S.qw3, 1)
+    TE.wait_ge(S.qge, 1)
+    TE.wait_ge(S.in2, 14)
+    mm(0, "w3", 0, "c", 0, S.fe)
+    TE.wait_ge(S.cr2, 32)
+    mm(1, "w3", 0, "e", 0, S.fc)
+    V.wait_ge(S.fe, 1)
+    y0 = W * mine0
+    if tail:
+        V.tensor_copy(T.yt[:, y0 + H - tail:y0 + H], T.ps[:, 0:tail]).then_inc(S.ye, 1)
+    V.tensor_copy(T.yt[:, y0:y0 + H - tail], T.ps[:, tail:H]).then_inc(S.ye, 1)
+    SY.wait_ge(S.ye, 2 if tail else 1)
+    SY.dma_start(T.y[:, y0:y0 + H], T.yt[:, y0:y0 + H]).then_inc(S.out, 16)
+    V.wait_ge(S.fc, 1)
+    V.tensor_copy(T.yt[:, W * far0:W * far0 + H], bank(1)).then_inc(S.yc, 1)
+    SY.wait_ge(S.yc, 1)
+    SY.dma_start(T.y[:, W * far0:W * far0 + H], T.yt[:, W * far0:W * far0 + H]).then_inc(S.out, 16)
+
+    sent = [0]
+
+    def cross(name, land, hop):
+        for codes in (True, False):
+            sent[0] += fused(g, core, T, topo, hop, [(kc if codes else sc, view(T, codes, name, a, 64), view(T, codes, land, 0, 64))
+                                                     for a, kc, sc in P["blocks"][rank]])
+
+    def inside(name, base, land, lbase, sem):
+        for codes in (True, False):
+            sent[0] += fused(g, core, T, topo, sem, [(cores[d], view(T, codes, name, base + W * p, W),
+                                                      view(T, codes, land, lbase + W * P["ring"][d].index(rank), W))
+                                                     for p, d in enumerate(ring)])
+
+    g.wait_ge(S.qha, 1)
+    cross("ha", "r1", S.hop1)
+    g.wait_ge(S.qhb, 1)
+    inside("b", 0, "b", IN1, S.in1)
+    g.wait_ge(S.qgx, 1)
+    cross("gx", "r2", S.hop2)
+    g.wait_ge(S.qge, 1)
+    inside("c", PK2 + W, "c", 0, S.in2)
+    g.wait_ge(S.sent, sent[0])
+    SY.wait_ge(S.out, 32)

@@ -3,6 +3,7 @@ from concourse.mybir import dt, AluOpType, ActivationFunctionType
 
 SIM = 512
 W = 16
+R = 4 * W
 H = 128
 OWN1 = H - W
 IN1 = H
@@ -21,7 +22,7 @@ SCRATCH = {
     "ps": ("psum", [128, 512 * 8], "float32"),
 }
 for _n, _w in (("xa", H), ("xb", H), ("w1", 256), ("w2", 256), ("w3", 128), ("ha", H), ("b", CR1 + H), ("c", PK2 + H),
-               ("gx", H), ("e", H), ("r1", 64), ("r2", 64)):
+               ("gx", H), ("e", H), ("r1", R), ("r2", R)):
     SCRATCH["k_" + _n] = ("sbuf", [128, _w], X4)
     SCRATCH["s_" + _n] = ("sbuf", [128, _w], "uint8")
 
@@ -40,23 +41,36 @@ def plan(T, topo):
     rk = [topo.rack(topo.host(c)) for c in cores]
     mine = [[r for r in ranks if rk[r] == rk[j]] for j in ranks]
     far = [[r for r in ranks if rk[r] != rk[j]] for j in ranks]
-    ring, blocks, relay = [], [], {}
+
+    def helpers(c):
+        chip = [d for d in range(SIM) if topo.host(d) == topo.host(c) and topo.chip(d) == topo.chip(c) and T.rank_of(d) is None]
+        return [d for d in chip if topo.die(d) == topo.die(c)], [d for d in chip if topo.die(d) != topo.die(c)]
+
+    hp = [helpers(c) for c in cores]
+    ring, blocks, yard, relay = [], [], [], {}
     for j in ranks:
         i = mine[j].index(j)
-        ring.append(mine[j][i + 1:] + mine[j][:i])
+        rg = mine[j][i + 1:] + mine[j][:i]
+        ring.append(rg)
         near = [r for r in far[j] if topo.may_write(cores[j], cores[r])]
         diag = [r for r in far[j] if r not in near]
-        peer = [cores[r] for r in near if topo.chip(cores[r]) == topo.chip(cores[j])][0]
-        help_ = [c for c in range(SIM) if topo.host(c) == topo.host(peer) and topo.chip(c) == topo.chip(peer)
-                 and topo.die(c) != topo.die(peer) and T.rank_of(c) is None]
+        same = [r for r in ranks if topo.chip(cores[r]) == topo.chip(cores[j]) and r != j]
+        pn = [r for r in near if r in same][0]
+        pd = [r for r in mine[j] if r in same][0]
         bl = []
-        for n, dests in enumerate((diag, near)):
-            kc, sc = help_[2 * n], help_[2 * n + 1]
-            relay[kc] = (j, dests, True)
-            relay[sc] = (j, dests, False)
+        for dests, kc, sc in ((diag, hp[pd][1][0], hp[pd][1][2]), (near, hp[pn][0][0], hp[pn][0][1])):
+            cut = [(d, W * n) for n, d in enumerate(dests)]
+            relay[kc] = (j, True, False, (cut, cut))
+            relay[sc] = (j, False, False, (cut, cut))
             bl.append((far[j].index(dests[0]) * W, kc, sc))
         blocks.append(bl)
-    PLAN.update(cores=cores, mine=mine, far=far, ring=ring, blocks=blocks, relay=relay)
+        one = [(d, W * n) for n, d in enumerate(rg)]
+        two = [(d, W * n + W) for n, d in enumerate(rg)]
+        ys = (hp[j][1][1], hp[j][1][3])
+        for n, c in enumerate(ys):
+            relay[c] = (j, True, True, tuple([(d, a - R * n) for d, a in p if R * n <= a < R * n + R] for p in (one, two)))
+        yard.append(ys)
+    PLAN.update(cores=cores, mine=mine, far=far, ring=ring, blocks=blocks, yard=yard, relay=relay)
     return PLAN
 
 
@@ -66,8 +80,7 @@ def view(T, codes, name, a, n):
     return T["s_" + name][:, a:a + n]
 
 
-def fused(g, core, T, topo, sem, moves):
-    m = 0xFFFF
+def fused(g, core, T, topo, sem, moves, m=0xFFFF):
     for d, _, _ in moves:
         m &= topo.mask(core, d)
     eng = [i for i in range(16) if m >> i & 1]
@@ -85,14 +98,21 @@ def fused(g, core, T, topo, sem, moves):
 
 
 def relay_program(g, core, T, topo, P):
-    j, dests, codes = P["relay"][core]
-    at = W * P["mine"][j].index(j)
-    sent = 0
-    for hop, land, buf, base, sem in ((T.sem.hop1, "r1", "b", CR1, T.sem.cr1), (T.sem.hop2, "r2", "e", 0, T.sem.cr2)):
-        g.wait_ge(hop, 4)
-        sent += fused(g, core, T, topo, sem, [(P["cores"][d], view(T, codes, land, W * n, W), view(T, codes, buf, base + at, W))
-                                              for n, d in enumerate(dests)])
-    g.wait_ge(T.sem.sent, sent)
+    j, codes, inside, cuts = P["relay"][core]
+    S, sent = T.sem, 0
+    off = topo.mask(core, P["relay"][core][3][0][0][0] if False else P["cores"][cuts[0][-1][0]])
+    for ph, cut in enumerate(cuts):
+        g.wait_ge((S.hop1, S.hop2)[ph], 4)
+        if inside:
+            buf, base, sem = (("b", IN1, S.in1), ("c", 0, S.in2))[ph]
+        else:
+            buf, base, sem = (("b", CR1, S.cr1), ("e", 0, S.cr2))[ph]
+        moves = []
+        for d, a in cut:
+            at = P["ring"][d].index(j) if inside else P["mine"][j].index(j)
+            moves.append((P["cores"][d], view(T, codes, ("r1", "r2")[ph], a, W), view(T, codes, buf, base + W * at, W)))
+        sent += fused(g, core, T, topo, sem, moves, off)
+    g.wait_ge(S.sent, sent)
 
 
 def rank_program(g, core, T, topo):
@@ -113,14 +133,15 @@ def rank_program(g, core, T, topo):
 
     A.dma_start(T.t10[:], T.w1[:, 0:512]).then_inc(S.lw10, 16)
     SY.dma_start(T.xa[:], T.x[:, 4 * W * far0:4 * W * far0 + 4 * H]).then_inc(S.lxa, 16)
-    A.dma_start(T.t11[:], T.w1[:, 512:1024]).then_inc(S.lw11, 16)
+    A.dma_start(T.t11[0:64, :], T.w1[0:64, 512:1024]).then_inc(S.lw11, 16)
+    SY.dma_start(T.t11[64:128, :], T.w1[64:128, 512:1024]).then_inc(S.lw11, 16)
     x0 = 4 * W * mine0
     nb = 16
     if tail:
         SY.dma_start(T.xb[:, 0:4 * tail], T.x[:, x0 + 4 * (H - tail):x0 + 4 * H]).then_inc(S.lxb, 16)
         nb = 32
     SY.dma_start(T.xb[:, 4 * tail:4 * H], T.x[:, x0:x0 + 4 * (H - tail)]).then_inc(S.lxb, 16)
-    SY.wait_ge(S.lw11, 16)
+    SY.wait_ge(S.lw11, 32)
     SY.wait_ge(S.lxb, nb)
     SY.dma_start(T.t2[:], T.w2[:]).then_inc(S.lw2, 16)
     SY.dma_start(T.t3[:], T.w3[:]).then_inc(S.lw3, 16)
@@ -148,7 +169,7 @@ def rank_program(g, core, T, topo):
     quant("w1", 0, 128, T.t10[:], S.qw10)
     V.wait_ge(S.lxa, 16)
     quant("xa", 0, H, T.xa[:], S.qxa)
-    V.wait_ge(S.lw11, 16)
+    V.wait_ge(S.lw11, 32)
     quant("w1", 128, 128, T.t11[:], S.qw11)
     TE.wait_ge(S.qw10, 1)
     TE.wait_ge(S.qxa, 1)
@@ -172,7 +193,7 @@ def rank_program(g, core, T, topo):
 
     TE.wait_ge(S.qw2, 2)
     TE.wait_ge(S.qhb, 1)
-    TE.wait_ge(S.in1, 14)
+    TE.wait_ge(S.in1, 21)
     mm(4, "w2", 0, "b", OWN1, S.ze0)
     mm(5, "w2", 128, "b", OWN1, S.ze1)
     acts(T.ge, 4, S.ze0, S.ze1, C2, S.te)
@@ -185,7 +206,7 @@ def rank_program(g, core, T, topo):
 
     TE.wait_ge(S.qw3, 1)
     TE.wait_ge(S.qge, 1)
-    TE.wait_ge(S.in2, 14)
+    TE.wait_ge(S.in2, 21)
     mm(0, "w3", 0, "c", 0, S.fe)
     TE.wait_ge(S.cr2, 32)
     mm(1, "w3", 0, "e", 0, S.fc)
@@ -202,25 +223,31 @@ def rank_program(g, core, T, topo):
     SY.dma_start(T.y[:, W * far0:W * far0 + H], T.yt[:, W * far0:W * far0 + H]).then_inc(S.out, 16)
 
     sent = [0]
+    off = topo.mask(core, cores[ring[0]])
 
     def cross(name, land, hop):
         for codes in (True, False):
-            sent[0] += fused(g, core, T, topo, hop, [(kc if codes else sc, view(T, codes, name, a, 64), view(T, codes, land, 0, 64))
+            sent[0] += fused(g, core, T, topo, hop, [(kc if codes else sc, view(T, codes, name, a, R), view(T, codes, land, 0, R))
                                                      for a, kc, sc in P["blocks"][rank]])
 
-    def inside(name, base, land, lbase, sem):
-        for codes in (True, False):
-            sent[0] += fused(g, core, T, topo, sem, [(cores[d], view(T, codes, name, base + W * p, W),
-                                                      view(T, codes, land, lbase + W * P["ring"][d].index(rank), W))
-                                                     for p, d in enumerate(ring)])
+    def in_codes(name, base, land, hop):
+        sent[0] += fused(g, core, T, topo, hop, [(c, view(T, True, name, base + R * n, R), view(T, True, land, 0, R))
+                                                 for n, c in enumerate(P["yard"][rank])], off)
+
+    def in_scales(name, base, land, lbase, sem):
+        sent[0] += fused(g, core, T, topo, sem, [(cores[d], view(T, False, name, base + W * p, W),
+                                                  view(T, False, land, lbase + W * P["ring"][d].index(rank), W))
+                                                 for p, d in enumerate(ring)])
 
     g.wait_ge(S.qha, 1)
     cross("ha", "r1", S.hop1)
     g.wait_ge(S.qhb, 1)
-    inside("b", 0, "b", IN1, S.in1)
+    in_codes("b", 0, "r1", S.hop1)
+    in_scales("b", 0, "b", IN1, S.in1)
+    g.wait_ge(S.qge, 1)
+    in_codes("c", PK2, "r2", S.hop2)
     g.wait_ge(S.qgx, 1)
     cross("gx", "r2", S.hop2)
-    g.wait_ge(S.qge, 1)
-    inside("c", PK2 + W, "c", 0, S.in2)
+    in_scales("c", PK2 + W, "c", 0, S.in2)
     g.wait_ge(S.sent, sent[0])
     SY.wait_ge(S.out, 32)

@@ -3,32 +3,31 @@ from concourse.mybir import dt, AluOpType, ActivationFunctionType
 
 SIM = 512
 W = 16
-R = 4 * W
+D = 2 * W
 H = 128
-OWN1 = H - W
-IN1 = H
-CR1 = IN1 + H - W
-PK2 = H - W
+HALF = H // 2
+OWN = H - D
+PK2 = H - D
+HP = 2 * H
 C1, C2 = 0.043, 0.041
 
 X4 = "float8_e4m3fn_x4"
 SCRATCH = {
-    "xa": ("sbuf", [128, 4 * H], "bfloat16"), "xb": ("sbuf", [128, 4 * H], "bfloat16"),
-    "t10": ("sbuf", [128, 512], "bfloat16"), "t11": ("sbuf", [128, 512], "bfloat16"),
-    "t2": ("sbuf", [128, 1024], "bfloat16"), "t3": ("sbuf", [128, 512], "bfloat16"),
-    "ha": ("sbuf", [128, 4 * H], "bfloat16"), "hb": ("sbuf", [128, 4 * H], "bfloat16"),
-    "ge": ("sbuf", [128, 4 * H], "bfloat16"), "gx": ("sbuf", [128, 4 * H], "bfloat16"),
+    "xp": ("sbuf", [128, 4 * H], "bfloat16"), "xr": ("sbuf", [128, 4 * H], "bfloat16"),
+    "t1": ("sbuf", [128, 1024], "bfloat16"), "t2": ("sbuf", [128, 1024], "bfloat16"), "t3": ("sbuf", [128, 512], "bfloat16"),
+    "hp": ("sbuf", [128, 4 * H], "bfloat16"), "hr": ("sbuf", [128, 4 * H], "bfloat16"),
+    "gt": ("sbuf", [128, 4 * H], "bfloat16"),
     "yt": ("sbuf", [128, 256], "float32"),
     "ps": ("psum", [128, 512 * 8], "float32"),
 }
-for _n, _w in (("xa", H), ("xb", H), ("w1", 256), ("w2", 256), ("w3", 128), ("ha", H), ("b", CR1 + H), ("c", PK2 + H),
-               ("gx", H), ("e", H), ("r1", R), ("r2", R)):
+for _n, _w in (("xp", H), ("xr", H), ("w1", 256), ("w2", 256), ("w3", 128), ("hp", H), ("b", 2 * H - D), ("c", PK2 + H),
+               ("e", H), ("u", HP + 2 * D), ("v", 256), ("g", H), ("r", 2 * D)):
     SCRATCH["k_" + _n] = ("sbuf", [128, _w], X4)
     SCRATCH["s_" + _n] = ("sbuf", [128, _w], "uint8")
 
-SEMAPHORES = ["lxa", "lxb", "lw10", "lw11", "lw2", "lw3", "qw10", "qw11", "qxa", "qxb", "qw2", "qw3",
-              "za0", "za1", "zb0", "zb1", "ze0", "ze1", "zc0", "zc1", "ta", "tb", "te", "tc", "qha", "qhb", "qge", "qgx",
-              "in1", "cr1", "in2", "cr2", "fe", "fc", "ye", "yc", "out", "sent", "hop1", "hop2"]
+SEMAPHORES = ["lw20", "lw21", "lw10", "lw11", "lxp", "lxr", "lw3", "qw2", "qw10", "qw11", "qxp", "qxr", "qw3", "zp0", "zp1",
+              "zr0", "zr1", "ze0", "ze1", "zf0", "zf1", "tp", "tr", "tg", "qhp", "qhr", "qg", "ms",
+              "wl0", "wl1", "wc", "wf", "hin", "gr", "gp", "hop", "fr", "fp", "yr", "yp", "out", "sent"]
 
 PLAN = {}
 
@@ -38,39 +37,27 @@ def plan(T, topo):
         return PLAN
     cores = [int(c) for c in T.cores]
     ranks = range(len(cores))
-    rk = [topo.rack(topo.host(c)) for c in cores]
-    mine = [[r for r in ranks if rk[r] == rk[j]] for j in ranks]
-    far = [[r for r in ranks if rk[r] != rk[j]] for j in ranks]
-
-    def helpers(c):
-        chip = [d for d in range(SIM) if topo.host(d) == topo.host(c) and topo.chip(d) == topo.chip(c) and T.rank_of(d) is None]
-        return [d for d in chip if topo.die(d) == topo.die(c)], [d for d in chip if topo.die(d) != topo.die(c)]
-
-    hp = [helpers(c) for c in cores]
-    ring, blocks, yard, relay = [], [], [], {}
+    host = [topo.host(c) for c in cores]
+    rk = [topo.rack(h) for h in host]
+    inn = [[r for r in ranks if host[r] == host[j]] for j in ranks]
+    oth = [[r for r in ranks if rk[r] == rk[j] and host[r] != host[j]] for j in ranks]
+    partner = [[r for r in ranks if rk[r] != rk[j] and topo.may_write(cores[j], cores[r])
+                and topo.chip(cores[r]) == topo.chip(cores[j])][0] for j in ranks]
+    ring, role, pc, kc = [], {}, [], []
     for j in ranks:
-        i = mine[j].index(j)
-        rg = mine[j][i + 1:] + mine[j][:i]
-        ring.append(rg)
-        near = [r for r in far[j] if topo.may_write(cores[j], cores[r])]
-        diag = [r for r in far[j] if r not in near]
-        same = [r for r in ranks if topo.chip(cores[r]) == topo.chip(cores[j]) and r != j]
-        pn = [r for r in near if r in same][0]
-        pd = [r for r in mine[j] if r in same][0]
-        bl = []
-        for dests, kc, sc in ((diag, hp[pd][1][0], hp[pd][1][2]), (near, hp[pn][0][0], hp[pn][0][1])):
-            cut = [(d, W * n) for n, d in enumerate(dests)]
-            relay[kc] = (j, True, False, (cut, cut))
-            relay[sc] = (j, False, False, (cut, cut))
-            bl.append((far[j].index(dests[0]) * W, kc, sc))
-        blocks.append(bl)
-        one = [(d, W * n) for n, d in enumerate(rg)]
-        two = [(d, W * n + W) for n, d in enumerate(rg)]
-        ys = (hp[j][1][1], hp[j][1][3])
-        for n, c in enumerate(ys):
-            relay[c] = (j, True, True, tuple([(d, a - R * n) for d, a in p if R * n <= a < R * n + R] for p in (one, two)))
-        yard.append(ys)
-    PLAN.update(cores=cores, mine=mine, far=far, ring=ring, blocks=blocks, yard=yard, relay=relay)
+        c = cores[j]
+        i = inn[j].index(j)
+        ring.append(inn[j][i + 1:] + inn[j][:i])
+        chip = [d for d in range(SIM) if topo.host(d) == topo.host(c) and topo.chip(d) == topo.chip(c) and T.rank_of(d) is None]
+        near = [d for d in chip if topo.die(d) == topo.die(c)]
+        away = [d for d in chip if topo.die(d) != topo.die(c)]
+        pc.append((away[0], away[2]))
+        kc.append(((near[1], away[1]), (near[2], away[3])))
+        for n in (0, 1):
+            role[pc[j][n]] = ("P", j, n)
+            role[kc[j][0][n]] = ("K", j, True, n)
+            role[kc[j][1][n]] = ("K", j, False, n)
+    PLAN.update(cores=cores, inn=inn, oth=oth, partner=partner, ring=ring, role=role, pc=pc, kc=kc)
     return PLAN
 
 
@@ -80,38 +67,102 @@ def view(T, codes, name, a, n):
     return T["s_" + name][:, a:a + n]
 
 
-def fused(g, core, T, topo, sem, moves, m=0xFFFF):
-    for d, _, _ in moves:
-        m &= topo.mask(core, d)
-    eng = [i for i in range(16) if m >> i & 1]
-    per = 1
-    while 2 * per * len(moves) <= len(eng):
-        per *= 2
-    tr = []
-    for n, (d, src, dst) in enumerate(moves):
+def engines(topo, core, dst):
+    m = topo.mask(core, dst)
+    return [i for i in range(16) if m >> i & 1]
+
+
+def fused(g, core, T, topo, moves):
+    tr, n = [], 0
+    for d, src, dst, eng, sem in moves:
         rid, pid = topo.addr(d, core)
-        tr.append(RemoteDMATransfer(dst_ids=[DstId(rid=rid, pnc=pid)],
-                                    dma_engine_mask=sum(1 << i for i in eng[n * per:n * per + per]),
+        tr.append(RemoteDMATransfer(dst_ids=[DstId(rid=rid, pnc=pid)], dma_engine_mask=sum(1 << i for i in eng),
                                     remote_sem=sem, src=src, dst=dst))
+        n += len(eng)
     g.remote_dma_fused(tr, local_sem=T.sem.sent)
-    return per * len(moves)
+    return n
 
 
-def relay_program(g, core, T, topo, P):
-    j, codes, inside, cuts = P["relay"][core]
-    S, sent = T.sem, 0
-    off = topo.mask(core, P["relay"][core][3][0][0][0] if False else P["cores"][cuts[0][-1][0]])
-    for ph, cut in enumerate(cuts):
-        g.wait_ge((S.hop1, S.hop2)[ph], 4)
-        if inside:
-            buf, base, sem = (("b", IN1, S.in1), ("c", 0, S.in2))[ph]
-        else:
-            buf, base, sem = (("b", CR1, S.cr1), ("e", 0, S.cr2))[ph]
-        moves = []
-        for d, a in cut:
-            at = P["ring"][d].index(j) if inside else P["mine"][j].index(j)
-            moves.append((P["cores"][d], view(T, codes, ("r1", "r2")[ph], a, W), view(T, codes, buf, base + W * at, W)))
-        sent += fused(g, core, T, topo, sem, moves, off)
+def bank(T, b, n=H):
+    return T.ps[:, 512 * b:512 * b + n]
+
+
+def mm(g, T, b, w, wa, x, xa, sem):
+    g.tensor.matmul_mx(bank(T, b), T["k_" + w][:, wa:wa + H], T["s_" + w][:, wa:wa + H],
+                       T["k_" + x][:, xa:xa + H], T["s_" + x][:, xa:xa + H], True, True).then_inc(sem, 1)
+
+
+def signs(g, T, scalar, tile, c, calls, done):
+    q = g.scalar if scalar else g.vector
+    for sem, src, at, end in calls:
+        if sem is not None:
+            q.wait_ge(sem, 1)
+        for s in (0, 1):
+            f = -c if s else c
+            out = tile[:, at + s:end:8]
+            if scalar:
+                q.activation(out, src, ActivationFunctionType.Relu, scale=f).then_inc(done, 1)
+            else:
+                q.tensor_scalar(out, src, f, 0.0, AluOpType.mult, AluOpType.max).then_inc(done, 1)
+
+
+def pair_tile(g, T, lo, width, done):
+    S = T.sem
+    for scalar, zs in ((False, (S.ze0, S.zf0)), (True, (S.ze1, S.zf1))):
+        signs(g, T, scalar, T.gt, C2,
+              [(zs[p], T.ps[:, 512 * (4 + 2 * p + int(scalar)) + lo + p:512 * (4 + 2 * p + int(scalar)) + H:2],
+                4 * p + 2 * int(scalar), 4 * width) for p in (0, 1)], done)
+    g.vector.wait_ge(done, 8)
+
+
+def hand_on(g, core, T, topo, P):
+    _, j, codes, n = P["role"][core]
+    q = P["inn"][j].index(j)
+    dests = [P["pc"][e][q // 2] for e in P["oth"][j][2 * n:2 * n + 2]]
+    eng = engines(topo, core, dests[0])
+    k = len(eng) // 2
+    g.wait_ge(T.sem.hop, 4)
+    sent = fused(g, core, T, topo, [(d, view(T, codes, "r", D * i, D), view(T, codes, "u", HP + D * (q % 2), D),
+                                     eng[k * i:k * i + k], T.sem.hin) for i, d in enumerate(dests)])
+    g.wait_ge(T.sem.sent, sent)
+
+
+def pair_program(g, core, T, topo, P):
+    _, e, n = P["role"][core]
+    S, V, TE = T.sem, g.vector, g.tensor
+    srcs = P["oth"][e][2 * n:2 * n + 2]
+    V.memset(T.gt[:, 8 * D:4 * H], 0.0).then_inc(S.ms, 1)
+
+    TE.wait_ge(S.wl1, 8)
+    TE.wait_ge(S.wl0, 8)
+    TE.wait_ge(S.hin, 16)
+    mm(g, T, 4, "u", 0, "u", HP + 2 * D - H, S.ze0)
+    mm(g, T, 5, "u", H, "u", HP + 2 * D - H, S.ze1)
+    TE.wait_ge(S.wc, 16)
+    TE.wait_ge(S.wf, 16)
+    mm(g, T, 6, "v", 0, "u", HP + 2 * D - H, S.zf0)
+    mm(g, T, 7, "v", H, "u", HP + 2 * D - H, S.zf1)
+    pair_tile(g, T, H - 2 * D, 2 * D, S.tg)
+    V.wait_ge(S.ms, 1)
+    V.quantize_mx(T.k_g[:], T.s_g[:], T.gt[:]).then_inc(S.qg, 1)
+
+    mate = P["pc"][P["partner"][e]][n]
+    eng = engines(topo, core, mate)
+    k = len(eng) // 2
+    at = H + HALF * n
+    sent = 0
+    g.wait_ge(S.wl1, 8)
+    for codes in (True, False):
+        sent += fused(g, core, T, topo, [(mate, view(T, codes, "u", at, HALF), view(T, codes, "v", at, HALF), eng, S.wc)])
+    g.wait_ge(S.wc, 16)
+    for codes in (True, False):
+        sent += fused(g, core, T, topo, [(d, view(T, codes, "v", at, HALF), view(T, codes, "v", at, HALF), eng[k * i:k * i + k], S.wf)
+                                         for i, d in enumerate((P["cores"][e], P["pc"][e][1 - n]))])
+    g.wait_ge(S.qg, 1)
+    for codes in (True, False):
+        sent += fused(g, core, T, topo, [(P["cores"][d], view(T, codes, "g", D * i, D),
+                                          view(T, codes, "e", D * P["oth"][d].index(e), D), eng[k * i:k * i + k], S.gp)
+                                         for i, d in enumerate(srcs)])
     g.wait_ge(S.sent, sent)
 
 
@@ -119,135 +170,145 @@ def rank_program(g, core, T, topo):
     P = plan(T, topo)
     rank = T.rank_of(core)
     if rank is None:
-        if core in P["relay"]:
-            relay_program(g, core, T, topo, P)
+        kind = P["role"].get(core, ("",))[0]
+        if kind == "K":
+            hand_on(g, core, T, topo, P)
+        if kind == "P":
+            pair_program(g, core, T, topo, P)
         return
     S = T.sem
-    cores, ring = P["cores"], P["ring"][rank]
-    far0, mine0 = P["far"][rank][0], P["mine"][rank][0]
-    me = P["mine"][rank].index(rank)
-    tail = H - W * (me + 1)
+    cores, ring, partner = P["cores"], P["ring"][rank], P["partner"]
+    q = P["inn"][rank].index(rank)
     V, TE, A, SY = g.vector, g.tensor, g.scalar, g.sync
-    mul, mx = AluOpType.mult, AluOpType.max
-    relu = ActivationFunctionType.Relu
+    runs_r = (P["inn"][rank][0], partner[P["inn"][rank][0]])
+    runs_p = (P["oth"][rank][0], partner[P["oth"][rank][0]])
+    segs = [(a, b) for a, b in ((q + 1, 4), (0, q + 1)) if b > a]
 
-    A.dma_start(T.t10[:], T.w1[:, 0:512]).then_inc(S.lw10, 16)
-    SY.dma_start(T.xa[:], T.x[:, 4 * W * far0:4 * W * far0 + 4 * H]).then_inc(S.lxa, 16)
-    A.dma_start(T.t11[0:64, :], T.w1[0:64, 512:1024]).then_inc(S.lw11, 16)
-    SY.dma_start(T.t11[64:128, :], T.w1[64:128, 512:1024]).then_inc(S.lw11, 16)
-    x0 = 4 * W * mine0
-    nb = 16
-    if tail:
-        SY.dma_start(T.xb[:, 0:4 * tail], T.x[:, x0 + 4 * (H - tail):x0 + 4 * H]).then_inc(S.lxb, 16)
-        nb = 32
-    SY.dma_start(T.xb[:, 4 * tail:4 * H], T.x[:, x0:x0 + 4 * (H - tail)]).then_inc(S.lxb, 16)
-    SY.wait_ge(S.lw11, 32)
-    SY.wait_ge(S.lxb, nb)
-    SY.dma_start(T.t2[:], T.w2[:]).then_inc(S.lw2, 16)
+    A.dma_start(T.t2[:, 0:512], T.w2[:, 0:512]).then_inc(S.lw20, 16)
+    SY.dma_start(T.t2[:, 512:1024], T.w2[:, 512:1024]).then_inc(S.lw21, 16)
+    A.dma_start(T.t1[:, 0:512], T.w1[:, 0:512]).then_inc(S.lw10, 16)
+    for p in (0, 1):
+        SY.dma_start(T.xp[:, 256 * p:256 * p + 256], T.x[:, 4 * W * runs_p[p]:4 * W * runs_p[p] + 256]).then_inc(S.lxp, 16)
+    A.dma_start(T.t1[:, 512:1024], T.w1[:, 512:1024]).then_inc(S.lw11, 16)
+    for p in (0, 1):
+        at = 256 * p
+        for a, b in segs:
+            SY.dma_start(T.xr[:, at:at + 4 * W * (b - a)],
+                         T.x[:, 4 * W * (runs_r[p] + a):4 * W * (runs_r[p] + b)]).then_inc(S.lxr, 16)
+            at += 4 * W * (b - a)
     SY.dma_start(T.t3[:], T.w3[:]).then_inc(S.lw3, 16)
 
-    def bank(b, n=H):
-        return T.ps[:, 512 * b:512 * b + n]
+    def quant(name, a, src, sem):
+        V.quantize_mx(T["k_" + name][:, a:a + H], T["s_" + name][:, a:a + H], src).then_inc(sem, 1)
 
-    def quant(name, a, n, src, sem):
-        V.quantize_mx(T["k_" + name][:, a:a + n], T["s_" + name][:, a:a + n], src).then_inc(sem, 1)
+    def h_tile(tile, b, z0, z1, done):
+        for scalar, z in ((False, z0), (True, z1)):
+            k = int(scalar)
+            signs(g, T, scalar, tile, C1, [(None if p else z, T.ps[:, 512 * (b + k) + 64 * p:512 * (b + k) + 64 * p + 64],
+                                            4 * p + 2 * k, 4 * H) for p in (0, 1)], done)
+        V.wait_ge(done, 8)
 
-    def mm(b, w, wa, x, xa, sem):
-        TE.matmul_mx(bank(b), T["k_" + w][:, wa:wa + 128], T["s_" + w][:, wa:wa + 128],
-                     T["k_" + x][:, xa:xa + H], T["s_" + x][:, xa:xa + H], True, True).then_inc(sem, 1)
-
-    def acts(tile, b, z0, z1, c, done):
-        V.wait_ge(z0, 1)
-        V.tensor_scalar(tile[:, 0:4 * H:4], bank(b), c, 0.0, mul, mx).then_inc(done, 1)
-        V.tensor_scalar(tile[:, 1:4 * H:4], bank(b), -c, 0.0, mul, mx).then_inc(done, 1)
-        A.wait_ge(z1, 1)
-        A.activation(tile[:, 2:4 * H:4], bank(b + 1), relu, scale=c).then_inc(done, 1)
-        A.activation(tile[:, 3:4 * H:4], bank(b + 1), relu, scale=-c).then_inc(done, 1)
-        V.wait_ge(done, 4)
-
+    V.wait_ge(S.lw20, 16)
+    quant("w2", 0, T.t2[:, 0:512], S.qw2)
+    V.wait_ge(S.lw21, 16)
+    quant("w2", H, T.t2[:, 512:1024], S.qw2)
     V.wait_ge(S.lw10, 16)
-    quant("w1", 0, 128, T.t10[:], S.qw10)
-    V.wait_ge(S.lxa, 16)
-    quant("xa", 0, H, T.xa[:], S.qxa)
-    V.wait_ge(S.lw11, 32)
-    quant("w1", 128, 128, T.t11[:], S.qw11)
+    quant("w1", 0, T.t1[:, 0:512], S.qw10)
+    V.wait_ge(S.lxp, 32)
+    quant("xp", 0, T.xp[:], S.qxp)
+    V.wait_ge(S.lw11, 16)
+    quant("w1", H, T.t1[:, 512:1024], S.qw11)
+    V.wait_ge(S.lxr, 32 * len(segs))
+    quant("xr", 0, T.xr[:], S.qxr)
     TE.wait_ge(S.qw10, 1)
-    TE.wait_ge(S.qxa, 1)
-    mm(0, "w1", 0, "xa", 0, S.za0)
+    TE.wait_ge(S.qxp, 1)
+    mm(g, T, 0, "w1", 0, "xp", 0, S.zp0)
     TE.wait_ge(S.qw11, 1)
-    mm(1, "w1", 128, "xa", 0, S.za1)
-    acts(T.ha, 0, S.za0, S.za1, C1, S.ta)
-    quant("ha", 0, H, T.ha[:], S.qha)
-    V.wait_ge(S.lxb, nb)
-    quant("xb", 0, H, T.xb[:], S.qxb)
-    TE.wait_ge(S.qxb, 1)
-    mm(2, "w1", 0, "xb", 0, S.zb0)
-    mm(3, "w1", 128, "xb", 0, S.zb1)
-    acts(T.hb, 2, S.zb0, S.zb1, C1, S.tb)
-    quant("b", 0, H, T.hb[:], S.qhb)
-    V.wait_ge(S.lw2, 16)
-    quant("w2", 0, 128, T.t2[:, 0:512], S.qw2)
-    quant("w2", 128, 128, T.t2[:, 512:1024], S.qw2)
+    mm(g, T, 1, "w1", H, "xp", 0, S.zp1)
+    TE.wait_ge(S.qxr, 1)
+    mm(g, T, 2, "w1", 0, "xr", 0, S.zr0)
+    mm(g, T, 3, "w1", H, "xr", 0, S.zr1)
+    h_tile(T.hp, 0, S.zp0, S.zp1, S.tp)
+    quant("hp", 0, T.hp[:], S.qhp)
+    h_tile(T.hr, 2, S.zr0, S.zr1, S.tr)
+    quant("b", 0, T.hr[:], S.qhr)
     V.wait_ge(S.lw3, 16)
-    quant("w3", 0, 128, T.t3[:], S.qw3)
+    quant("w3", 0, T.t3[:], S.qw3)
 
     TE.wait_ge(S.qw2, 2)
-    TE.wait_ge(S.qhb, 1)
-    TE.wait_ge(S.in1, 21)
-    mm(4, "w2", 0, "b", OWN1, S.ze0)
-    mm(5, "w2", 128, "b", OWN1, S.ze1)
-    acts(T.ge, 4, S.ze0, S.ze1, C2, S.te)
-    quant("c", PK2, H, T.ge[:], S.qge)
-    TE.wait_ge(S.cr1, 32)
-    mm(6, "w2", 0, "b", CR1, S.zc0)
-    mm(7, "w2", 128, "b", CR1, S.zc1)
-    acts(T.gx, 6, S.zc0, S.zc1, C2, S.tc)
-    quant("gx", 0, H, T.gx[:], S.qgx)
+    TE.wait_ge(S.qhr, 1)
+    TE.wait_ge(S.hin, 12)
+    mm(g, T, 4, "w2", 0, "b", OWN, S.ze0)
+    mm(g, T, 5, "w2", H, "b", OWN, S.ze1)
+    TE.wait_ge(S.wc, 4)
+    mm(g, T, 6, "v", 0, "b", OWN, S.zf0)
+    TE.wait_ge(S.wf, 16)
+    mm(g, T, 7, "v", H, "b", OWN, S.zf1)
+    pair_tile(g, T, 0, H, S.tg)
+    quant("c", PK2, T.gt[:], S.qg)
 
     TE.wait_ge(S.qw3, 1)
-    TE.wait_ge(S.qge, 1)
-    TE.wait_ge(S.in2, 21)
-    mm(0, "w3", 0, "c", 0, S.fe)
-    TE.wait_ge(S.cr2, 32)
-    mm(1, "w3", 0, "e", 0, S.fc)
-    V.wait_ge(S.fe, 1)
-    y0 = W * mine0
-    if tail:
-        V.tensor_copy(T.yt[:, y0 + H - tail:y0 + H], T.ps[:, 0:tail]).then_inc(S.ye, 1)
-    V.tensor_copy(T.yt[:, y0:y0 + H - tail], T.ps[:, tail:H]).then_inc(S.ye, 1)
-    SY.wait_ge(S.ye, 2 if tail else 1)
-    SY.dma_start(T.y[:, y0:y0 + H], T.yt[:, y0:y0 + H]).then_inc(S.out, 16)
-    V.wait_ge(S.fc, 1)
-    V.tensor_copy(T.yt[:, W * far0:W * far0 + H], bank(1)).then_inc(S.yc, 1)
-    SY.wait_ge(S.yc, 1)
-    SY.dma_start(T.y[:, W * far0:W * far0 + H], T.yt[:, W * far0:W * far0 + H]).then_inc(S.out, 16)
+    TE.wait_ge(S.qg, 1)
+    TE.wait_ge(S.gr, 12)
+    mm(g, T, 0, "w3", 0, "c", 0, S.fr)
+    TE.wait_ge(S.gp, 32)
+    mm(g, T, 1, "w3", 0, "e", 0, S.fp)
+    V.wait_ge(S.fr, 1)
+    for p in (0, 1):
+        at = 0
+        for a, b in segs:
+            V.tensor_copy(T.yt[:, W * (runs_r[p] + a):W * (runs_r[p] + b)],
+                          T.ps[:, at + p:at + D * (b - a):2]).then_inc(S.yr, 1)
+            at += D * (b - a)
+    SY.wait_ge(S.yr, 2 * len(segs))
+    for p in (0, 1):
+        o = W * runs_r[p]
+        SY.dma_start(T.y[:, o:o + 64], T.yt[:, o:o + 64]).then_inc(S.out, 16)
+    A.wait_ge(S.fp, 1)
+    for p in (0, 1):
+        o = W * runs_p[p]
+        A.activation(T.yt[:, o:o + 64], T.ps[:, 512 + p:512 + H:2], ActivationFunctionType.Copy).then_inc(S.yp, 1)
+    A.wait_ge(S.yp, 2)
+    o = W * runs_p[0]
+    A.dma_start(T.y[:, o:o + 64], T.yt[:, o:o + 64]).then_inc(S.out, 16)
+    SY.wait_ge(S.yp, 2)
+    o = W * runs_p[1]
+    SY.dma_start(T.y[:, o:o + 64], T.yt[:, o:o + 64]).then_inc(S.out, 16)
 
-    sent = [0]
-    off = topo.mask(core, cores[ring[0]])
+    sent = 0
+    far = cores[partner[rank]]
+    off = engines(topo, core, far)
+    on = [i for i in engines(topo, core, P["pc"][rank][0]) if i not in off]
+    half = len(on) // 2
 
-    def cross(name, land, hop):
+    def to_p(codes, name, a, land, sem):
+        return [(P["pc"][rank][n], view(T, codes, name, a, H), view(T, codes, land, a, H), on[half * n:half * n + half], sem)
+                for n in (0, 1)]
+
+    def direct(name, base, land, lbase, sem):
+        n = 0
         for codes in (True, False):
-            sent[0] += fused(g, core, T, topo, hop, [(kc if codes else sc, view(T, codes, name, a, R), view(T, codes, land, 0, R))
-                                                     for a, kc, sc in P["blocks"][rank]])
+            n += fused(g, core, T, topo, [(cores[d], view(T, codes, name, base + D * i, D),
+                                           view(T, codes, land, lbase + D * P["ring"][d].index(rank), D),
+                                           off[2 + 2 * i:4 + 2 * i], sem) for i, d in enumerate(ring)])
+        return n
 
-    def in_codes(name, base, land, hop):
-        sent[0] += fused(g, core, T, topo, hop, [(c, view(T, True, name, base + R * n, R), view(T, True, land, 0, R))
-                                                 for n, c in enumerate(P["yard"][rank])], off)
-
-    def in_scales(name, base, land, lbase, sem):
-        sent[0] += fused(g, core, T, topo, sem, [(cores[d], view(T, False, name, base + W * p, W),
-                                                  view(T, False, land, lbase + W * P["ring"][d].index(rank), W))
-                                                 for p, d in enumerate(ring)])
-
-    g.wait_ge(S.qha, 1)
-    cross("ha", "r1", S.hop1)
-    g.wait_ge(S.qhb, 1)
-    in_codes("b", 0, "r1", S.hop1)
-    in_scales("b", 0, "b", IN1, S.in1)
-    g.wait_ge(S.qge, 1)
-    in_codes("c", PK2, "r2", S.hop2)
-    g.wait_ge(S.qgx, 1)
-    cross("gx", "r2", S.hop2)
-    in_scales("c", PK2 + W, "c", 0, S.in2)
-    g.wait_ge(S.sent, sent[0])
-    SY.wait_ge(S.out, 32)
+    g.wait_ge(S.qw2, 2)
+    for codes, ce in ((True, off[0:2]), (False, off[2:4])):
+        sent += fused(g, core, T, topo, [(far, view(T, codes, "w2", 0, H), view(T, codes, "v", 0, H), ce, S.wc)]
+                      + to_p(codes, "w2", H, "u", S.wl1))
+    for codes in (True, False):
+        sent += fused(g, core, T, topo, to_p(codes, "w2", 0, "u", S.wl0))
+    g.wait_ge(S.qhp, 1)
+    for codes in (True, False):
+        sent += fused(g, core, T, topo, [(P["kc"][rank][0 if codes else 1][n], view(T, codes, "hp", 2 * D * n, 2 * D),
+                                          view(T, codes, "r", 0, 2 * D), on[half * n:half * n + half], S.hop) for n in (0, 1)])
+    g.wait_ge(S.qhr, 1)
+    sent += direct("b", 0, "b", H, S.hin)
+    g.wait_ge(S.wc, 4)
+    for codes in (True, False):
+        sent += fused(g, core, T, topo, to_p(codes, "v", 0, "v", S.wf))
+    g.wait_ge(S.qg, 1)
+    sent += direct("c", PK2 + D, "c", 0, S.gr)
+    g.wait_ge(S.sent, sent)
+    SY.wait_ge(S.out, 64)

from concourse.bass import DstId, RemoteDMATransfer
from concourse.mybir import dt, AluOpType, ActivationFunctionType

SIM = 512
W = 16
D = 2 * W
H = 128
HALF = H // 2
OWN = H - D
PK2 = H - D
HP = 2 * H
C1, C2 = 0.043, 0.041

X4 = "float8_e4m3fn_x4"
SCRATCH = {
    "xp": ("sbuf", [128, 4 * H], "bfloat16"), "xr": ("sbuf", [128, 4 * H], "bfloat16"),
    "t1": ("sbuf", [128, 1024], "bfloat16"), "t2": ("sbuf", [128, 1024], "bfloat16"), "t3": ("sbuf", [128, 512], "bfloat16"),
    "hp": ("sbuf", [128, 4 * H], "bfloat16"), "hr": ("sbuf", [128, 4 * H], "bfloat16"),
    "gt": ("sbuf", [128, 4 * H], "bfloat16"),
    "yt": ("sbuf", [128, 256], "float32"),
    "ps": ("psum", [128, 512 * 8], "float32"),
}
for _n, _w in (("xp", H), ("xr", H), ("w1", 256), ("w2", 256), ("w3", 128), ("hp", H), ("b", 2 * H - D), ("c", PK2 + H),
               ("e", H), ("u", HP + 2 * D), ("v", 256), ("g", H), ("r", 2 * D)):
    SCRATCH["k_" + _n] = ("sbuf", [128, _w], X4)
    SCRATCH["s_" + _n] = ("sbuf", [128, _w], "uint8")

SEMAPHORES = ["lw20", "lw21", "lw10", "lw11", "lxp", "lxr", "lw3", "qw2", "qw10", "qw11", "qxp", "qxr", "qw3", "zp0", "zp1",
              "zr0", "zr1", "ze0", "ze1", "zf0", "zf1", "tp", "tr", "tg", "qhp", "qhr", "qg", "ms",
              "wl0", "wl1", "wc", "wf", "hin", "gr", "gp", "hop", "fr", "fp", "yr", "yp", "out", "sent"]

PLAN = {}


def plan(T, topo):
    if PLAN:
        return PLAN
    cores = [int(c) for c in T.cores]
    ranks = range(len(cores))
    host = [topo.host(c) for c in cores]
    rk = [topo.rack(h) for h in host]
    inn = [[r for r in ranks if host[r] == host[j]] for j in ranks]
    oth = [[r for r in ranks if rk[r] == rk[j] and host[r] != host[j]] for j in ranks]
    partner = [[r for r in ranks if rk[r] != rk[j] and topo.may_write(cores[j], cores[r])
                and topo.chip(cores[r]) == topo.chip(cores[j])][0] for j in ranks]
    ring, role, pc, kc = [], {}, [], []
    for j in ranks:
        c = cores[j]
        i = inn[j].index(j)
        ring.append(inn[j][i + 1:] + inn[j][:i])
        chip = [d for d in range(SIM) if topo.host(d) == topo.host(c) and topo.chip(d) == topo.chip(c) and T.rank_of(d) is None]
        near = [d for d in chip if topo.die(d) == topo.die(c)]
        away = [d for d in chip if topo.die(d) != topo.die(c)]
        pc.append((away[0], away[2]))
        kc.append(((near[1], away[1]), (near[2], away[3])))
        for n in (0, 1):
            role[pc[j][n]] = ("P", j, n)
            role[kc[j][0][n]] = ("K", j, True, n)
            role[kc[j][1][n]] = ("K", j, False, n)
    PLAN.update(cores=cores, inn=inn, oth=oth, partner=partner, ring=ring, role=role, pc=pc, kc=kc)
    return PLAN


def view(T, codes, name, a, n):
    if codes:
        return T["k_" + name][:, a:a + n].bitcast(dt.uint8)
    return T["s_" + name][:, a:a + n]


def engines(topo, core, dst):
    m = topo.mask(core, dst)
    return [i for i in range(16) if m >> i & 1]


def fused(g, core, T, topo, moves):
    tr, n = [], 0
    for d, src, dst, eng, sem in moves:
        rid, pid = topo.addr(d, core)
        tr.append(RemoteDMATransfer(dst_ids=[DstId(rid=rid, pnc=pid)], dma_engine_mask=sum(1 << i for i in eng),
                                    remote_sem=sem, src=src, dst=dst))
        n += len(eng)
    g.remote_dma_fused(tr, local_sem=T.sem.sent)
    return n


def bank(T, b, n=H):
    return T.ps[:, 512 * b:512 * b + n]


def mm(g, T, b, w, wa, x, xa, sem):
    g.tensor.matmul_mx(bank(T, b), T["k_" + w][:, wa:wa + H], T["s_" + w][:, wa:wa + H],
                       T["k_" + x][:, xa:xa + H], T["s_" + x][:, xa:xa + H], True, True).then_inc(sem, 1)


def signs(g, T, scalar, tile, c, calls, done):
    q = g.scalar if scalar else g.vector
    for sem, src, at, end in calls:
        if sem is not None:
            q.wait_ge(sem, 1)
        for s in (0, 1):
            f = -c if s else c
            out = tile[:, at + s:end:8]
            if scalar:
                q.activation(out, src, ActivationFunctionType.Relu, scale=f).then_inc(done, 1)
            else:
                q.tensor_scalar(out, src, f, 0.0, AluOpType.mult, AluOpType.max).then_inc(done, 1)


def pair_tile(g, T, lo, width, done):
    S = T.sem
    for scalar, zs in ((False, (S.ze0, S.zf0)), (True, (S.ze1, S.zf1))):
        signs(g, T, scalar, T.gt, C2,
              [(zs[p], T.ps[:, 512 * (4 + 2 * p + int(scalar)) + lo + p:512 * (4 + 2 * p + int(scalar)) + H:2],
                4 * p + 2 * int(scalar), 4 * width) for p in (0, 1)], done)
    g.vector.wait_ge(done, 8)


def hand_on(g, core, T, topo, P):
    _, j, codes, n = P["role"][core]
    q = P["inn"][j].index(j)
    dests = [P["pc"][e][q // 2] for e in P["oth"][j][2 * n:2 * n + 2]]
    eng = engines(topo, core, dests[0])
    k = len(eng) // 2
    g.wait_ge(T.sem.hop, 4)
    sent = fused(g, core, T, topo, [(d, view(T, codes, "r", D * i, D), view(T, codes, "u", HP + D * (q % 2), D),
                                     eng[k * i:k * i + k], T.sem.hin) for i, d in enumerate(dests)])
    g.wait_ge(T.sem.sent, sent)


def pair_program(g, core, T, topo, P):
    _, e, n = P["role"][core]
    S, V, TE = T.sem, g.vector, g.tensor
    srcs = P["oth"][e][2 * n:2 * n + 2]
    V.memset(T.gt[:, 8 * D:4 * H], 0.0).then_inc(S.ms, 1)

    TE.wait_ge(S.wl1, 8)
    TE.wait_ge(S.wl0, 8)
    TE.wait_ge(S.hin, 16)
    mm(g, T, 4, "u", 0, "u", HP + 2 * D - H, S.ze0)
    mm(g, T, 5, "u", H, "u", HP + 2 * D - H, S.ze1)
    TE.wait_ge(S.wc, 16)
    TE.wait_ge(S.wf, 16)
    mm(g, T, 6, "v", 0, "u", HP + 2 * D - H, S.zf0)
    mm(g, T, 7, "v", H, "u", HP + 2 * D - H, S.zf1)
    pair_tile(g, T, H - 2 * D, 2 * D, S.tg)
    V.wait_ge(S.ms, 1)
    V.quantize_mx(T.k_g[:], T.s_g[:], T.gt[:]).then_inc(S.qg, 1)

    mate = P["pc"][P["partner"][e]][n]
    eng = engines(topo, core, mate)
    k = len(eng) // 2
    at = H + HALF * n
    sent = 0
    g.wait_ge(S.wl1, 8)
    for codes in (True, False):
        sent += fused(g, core, T, topo, [(mate, view(T, codes, "u", at, HALF), view(T, codes, "v", at, HALF), eng, S.wc)])
    g.wait_ge(S.wc, 16)
    for codes in (True, False):
        sent += fused(g, core, T, topo, [(d, view(T, codes, "v", at, HALF), view(T, codes, "v", at, HALF), eng[k * i:k * i + k], S.wf)
                                         for i, d in enumerate((P["cores"][e], P["pc"][e][1 - n]))])
    g.wait_ge(S.qg, 1)
    for codes in (True, False):
        sent += fused(g, core, T, topo, [(P["cores"][d], view(T, codes, "g", D * i, D),
                                          view(T, codes, "e", D * P["oth"][d].index(e), D), eng[k * i:k * i + k], S.gp)
                                         for i, d in enumerate(srcs)])
    g.wait_ge(S.sent, sent)


def rank_program(g, core, T, topo):
    P = plan(T, topo)
    rank = T.rank_of(core)
    if rank is None:
        kind = P["role"].get(core, ("",))[0]
        if kind == "K":
            hand_on(g, core, T, topo, P)
        if kind == "P":
            pair_program(g, core, T, topo, P)
        return
    S = T.sem
    cores, ring, partner = P["cores"], P["ring"][rank], P["partner"]
    q = P["inn"][rank].index(rank)
    V, TE, A, SY = g.vector, g.tensor, g.scalar, g.sync
    runs_r = (P["inn"][rank][0], partner[P["inn"][rank][0]])
    runs_p = (P["oth"][rank][0], partner[P["oth"][rank][0]])
    segs = [(a, b) for a, b in ((q + 1, 4), (0, q + 1)) if b > a]

    A.dma_start(T.t2[:, 0:512], T.w2[:, 0:512]).then_inc(S.lw20, 16)
    SY.dma_start(T.t2[:, 512:1024], T.w2[:, 512:1024]).then_inc(S.lw21, 16)
    A.dma_start(T.t1[:, 0:512], T.w1[:, 0:512]).then_inc(S.lw10, 16)
    for p in (0, 1):
        SY.dma_start(T.xp[:, 256 * p:256 * p + 256], T.x[:, 4 * W * runs_p[p]:4 * W * runs_p[p] + 256]).then_inc(S.lxp, 16)
    A.dma_start(T.t1[:, 512:1024], T.w1[:, 512:1024]).then_inc(S.lw11, 16)
    for p in (0, 1):
        at = 256 * p
        for a, b in segs:
            SY.dma_start(T.xr[:, at:at + 4 * W * (b - a)],
                         T.x[:, 4 * W * (runs_r[p] + a):4 * W * (runs_r[p] + b)]).then_inc(S.lxr, 16)
            at += 4 * W * (b - a)
    SY.dma_start(T.t3[:], T.w3[:]).then_inc(S.lw3, 16)

    def quant(name, a, src, sem):
        V.quantize_mx(T["k_" + name][:, a:a + H], T["s_" + name][:, a:a + H], src).then_inc(sem, 1)

    def h_tile(tile, b, z0, z1, done):
        for scalar, z in ((False, z0), (True, z1)):
            k = int(scalar)
            signs(g, T, scalar, tile, C1, [(None if p else z, T.ps[:, 512 * (b + k) + 64 * p:512 * (b + k) + 64 * p + 64],
                                            4 * p + 2 * k, 4 * H) for p in (0, 1)], done)
        V.wait_ge(done, 8)

    V.wait_ge(S.lw20, 16)
    quant("w2", 0, T.t2[:, 0:512], S.qw2)
    V.wait_ge(S.lw21, 16)
    quant("w2", H, T.t2[:, 512:1024], S.qw2)
    V.wait_ge(S.lw10, 16)
    quant("w1", 0, T.t1[:, 0:512], S.qw10)
    V.wait_ge(S.lxp, 32)
    quant("xp", 0, T.xp[:], S.qxp)
    V.wait_ge(S.lw11, 16)
    quant("w1", H, T.t1[:, 512:1024], S.qw11)
    V.wait_ge(S.lxr, 32 * len(segs))
    quant("xr", 0, T.xr[:], S.qxr)
    TE.wait_ge(S.qw10, 1)
    TE.wait_ge(S.qxp, 1)
    mm(g, T, 0, "w1", 0, "xp", 0, S.zp0)
    TE.wait_ge(S.qw11, 1)
    mm(g, T, 1, "w1", H, "xp", 0, S.zp1)
    TE.wait_ge(S.qxr, 1)
    mm(g, T, 2, "w1", 0, "xr", 0, S.zr0)
    mm(g, T, 3, "w1", H, "xr", 0, S.zr1)
    h_tile(T.hp, 0, S.zp0, S.zp1, S.tp)
    quant("hp", 0, T.hp[:], S.qhp)
    h_tile(T.hr, 2, S.zr0, S.zr1, S.tr)
    quant("b", 0, T.hr[:], S.qhr)
    V.wait_ge(S.lw3, 16)
    quant("w3", 0, T.t3[:], S.qw3)

    TE.wait_ge(S.qw2, 2)
    TE.wait_ge(S.qhr, 1)
    TE.wait_ge(S.hin, 12)
    mm(g, T, 4, "w2", 0, "b", OWN, S.ze0)
    mm(g, T, 5, "w2", H, "b", OWN, S.ze1)
    TE.wait_ge(S.wc, 4)
    mm(g, T, 6, "v", 0, "b", OWN, S.zf0)
    TE.wait_ge(S.wf, 16)
    mm(g, T, 7, "v", H, "b", OWN, S.zf1)
    pair_tile(g, T, 0, H, S.tg)
    quant("c", PK2, T.gt[:], S.qg)

    TE.wait_ge(S.qw3, 1)
    TE.wait_ge(S.qg, 1)
    TE.wait_ge(S.gr, 12)
    mm(g, T, 0, "w3", 0, "c", 0, S.fr)
    TE.wait_ge(S.gp, 32)
    mm(g, T, 1, "w3", 0, "e", 0, S.fp)
    V.wait_ge(S.fr, 1)
    for p in (0, 1):
        at = 0
        for a, b in segs:
            V.tensor_copy(T.yt[:, W * (runs_r[p] + a):W * (runs_r[p] + b)],
                          T.ps[:, at + p:at + D * (b - a):2]).then_inc(S.yr, 1)
            at += D * (b - a)
    SY.wait_ge(S.yr, 2 * len(segs))
    for p in (0, 1):
        o = W * runs_r[p]
        SY.dma_start(T.y[:, o:o + 64], T.yt[:, o:o + 64]).then_inc(S.out, 16)
    A.wait_ge(S.fp, 1)
    for p in (0, 1):
        o = W * runs_p[p]
        A.activation(T.yt[:, o:o + 64], T.ps[:, 512 + p:512 + H:2], ActivationFunctionType.Copy).then_inc(S.yp, 1)
    A.wait_ge(S.yp, 2)
    o = W * runs_p[0]
    A.dma_start(T.y[:, o:o + 64], T.yt[:, o:o + 64]).then_inc(S.out, 16)
    SY.wait_ge(S.yp, 2)
    o = W * runs_p[1]
    SY.dma_start(T.y[:, o:o + 64], T.yt[:, o:o + 64]).then_inc(S.out, 16)

    sent = 0
    far = cores[partner[rank]]
    off = engines(topo, core, far)
    on = [i for i in engines(topo, core, P["pc"][rank][0]) if i not in off]
    half = len(on) // 2

    def to_p(codes, name, a, land, sem):
        return [(P["pc"][rank][n], view(T, codes, name, a, H), view(T, codes, land, a, H), on[half * n:half * n + half], sem)
                for n in (0, 1)]

    def direct(name, base, land, lbase, sem):
        n = 0
        for codes in (True, False):
            n += fused(g, core, T, topo, [(cores[d], view(T, codes, name, base + D * i, D),
                                           view(T, codes, land, lbase + D * P["ring"][d].index(rank), D),
                                           off[2 + 2 * i:4 + 2 * i], sem) for i, d in enumerate(ring)])
        return n

    g.wait_ge(S.qw2, 2)
    for codes, ce in ((True, off[0:2]), (False, off[2:4])):
        sent += fused(g, core, T, topo, [(far, view(T, codes, "w2", 0, H), view(T, codes, "v", 0, H), ce, S.wc)]
                      + to_p(codes, "w2", H, "u", S.wl1))
    for codes in (True, False):
        sent += fused(g, core, T, topo, to_p(codes, "w2", 0, "u", S.wl0))
    g.wait_ge(S.qhp, 1)
    for codes in (True, False):
        sent += fused(g, core, T, topo, [(P["kc"][rank][0 if codes else 1][n], view(T, codes, "hp", 2 * D * n, 2 * D),
                                          view(T, codes, "r", 0, 2 * D), on[half * n:half * n + half], S.hop) for n in (0, 1)])
    g.wait_ge(S.qhr, 1)
    sent += direct("b", 0, "b", H, S.hin)
    g.wait_ge(S.wc, 4)
    for codes in (True, False):
        sent += fused(g, core, T, topo, to_p(codes, "v", 0, "v", S.wf))
    g.wait_ge(S.qg, 1)
    sent += direct("c", PK2 + D, "c", 0, S.gr)
    g.wait_ge(S.sent, sent)
    SY.wait_ge(S.out, 64)
